import numpy as np
import ml_dtypes


def mxq(x, axis, fmt="e4m3"):
    dtype, down = {"e4m3": (ml_dtypes.float8_e4m3fn, 7), "e5m2": (ml_dtypes.float8_e5m2, 14)}[fmt]
    v = np.moveaxis(np.asarray(x, np.float32).astype(ml_dtypes.bfloat16).astype(np.float64), axis, -1)
    blocks = v.reshape(v.shape[:-1] + (-1, 32))
    amax = np.abs(blocks).max(-1, keepdims=True)
    byte = np.maximum(np.where(amax > 0, np.frexp(amax)[1] - 1 + 127, 0) - down, 1)
    scale = np.exp2(byte - 127.0)
    codes = (blocks / scale).astype(np.float32).astype(dtype).astype(np.float64)
    return np.moveaxis((codes * scale).reshape(v.shape), -1, axis)


WIDE = False


def mx_kscale(k):
    if not WIDE:
        return np.ones(k)
    levels = np.array([10, -10, 5, -5, 0])
    if k % 512:
        return np.exp2(np.random.permutation(np.resize(levels, k // 32))).repeat(32)
    a = np.empty((k // 512, 16))
    for p in range(k // 512):
        a[p, :8] = np.random.permutation(np.resize(levels, 8))
        for g in range(8):
            far = levels[np.abs(levels - a[p, g]) >= 10]
            a[p, g + 8] = far[np.random.randint(len(far))]
    return np.exp2(a.ravel()).repeat(32)


def f64(x):
    return np.asarray(x).astype(np.float64)


def striped(idx):
    return np.tile(idx.reshape(-1, 16).T, (8, 1)).astype(np.uint16)


def unstriped(offs):
    return offs[:16].T.reshape(-1).astype(np.int64)


def relu(v):
    return np.maximum(v, 0.0)


K, T, E, C, N = 1024, 512, 8, 128, 512
M = 256


def by_expert(wq, xq):
    return np.concatenate([wq[e].T @ xq[:, e * C:(e + 1) * C] for e in range(E)], axis=1)


def setup_inputs():
    n = np.random.standard_normal
    s = mx_kscale(K)[:, None]
    v = mx_kscale(N)
    first = np.random.permutation(np.repeat(np.arange(E), T // E))
    second = (first + 1 + np.random.permutation(np.repeat(np.arange(E - 1), -(-T // (E - 1)))[:T])) % E
    while np.bincount(second, minlength=E).max() != T // E:
        load = np.bincount(second, minlength=E); hi, lo = int(load.argmax()), int(load.argmin())
        t = np.flatnonzero((second == hi) & (first != lo))[0]; second[t] = lo
    slot_token = np.empty(E * C, np.int64); pos = np.empty((2, T), np.int64); fill = np.zeros(E, np.int64)
    place = np.stack([np.random.permutation(C) for _ in range(E)])
    for r, deal in enumerate((first, second)):
        for t in np.random.permutation(T):
            e = deal[t]; j = e * C + place[e, fill[e]]; fill[e] += 1; slot_token[j] = t; pos[r, t] = j
    g = np.random.uniform(0.2, 0.8, T)
    return {
        "xT": (n((K, T)) * s).astype(np.float32),
        "w": (n((E, K, N)) / np.sqrt(K) / s[None] * v[None, None, :]).astype(np.float32),
        "b": (0.3 * n((N, E)) * v[:, None]).astype(np.float32),
        "wp": (n((N, M)) / np.sqrt(N) / v[:, None]).astype(np.float32),
        "gate": np.stack([np.tile(g, (N, 1)), np.tile(1.0 - g, (N, 1))]).astype(np.float32),
        "offs": striped(slot_token),
        "pos1": striped(pos[0]),
        "pos2": striped(pos[1]),
    }


def reference(xT, w, b, wp, gate, offs, pos1, pos2):
    idx = unstriped(offs)
    xq = mxq(f64(xT)[:, idx], 0, "e4m3")
    y = by_expert(mxq(f64(w), 1, "e4m3"), xq)
    y = relu(y + np.repeat(f64(b), C, axis=1))
    c = f64(gate[0]) * y[:, unstriped(pos1)] + f64(gate[1]) * y[:, unstriped(pos2)]
    return mxq(f64(wp), 0, "e4m3").T @ mxq(c, 0, "e4m3")

@@ -1,0 +1,261 @@
+from contextlib import ExitStack
+
+import concourse.mybir as mybir
+
+E, K, N, T, C, M = 8, 1024, 512, 512, 128, 256
+S = E * C
+P = 128
+J = 4
+TT = 4
+G = 32
+I = 4
+
+F32 = mybir.dt.float32
+BF16 = mybir.dt.bfloat16
+U32 = mybir.dt.uint32
+U16 = mybir.dt.uint16
+U8 = mybir.dt.uint8
+FP8X4 = mybir.dt.float8_e4m3fn_x4
+RELU = mybir.ActivationFunctionType.Relu
+MULT = mybir.AluOpType.mult
+ADD = mybir.AluOpType.add
+
+FLOPS = 2 * S * K * N + 2 * N * M * T
+BYTES = 4 * (K * T + E * K * N + N * E + N * M + 2 * T + M * T) + 2 * P * (S + 2 * T) // 16
+
+PIECES = 2 * E
+AHEAD = 10
+SLOT_CUTS = ((0, 384), (384, 768), (768, 1024))
+TOKEN_CUTS = ((0, 384), (384, 512))
+RUNS = (((0, 256), (256, 128)), ((384, 128),))
+
+
+def tile_moe_nxt_lin_relu_kernel(tc, xT, w, b, wp, gate, offs, pos1, pos2, out):
+    nc = tc.nc
+    with ExitStack() as ctx:
+        keep = ctx.enter_context(tc.tile_pool(name="keep", bufs=1))
+        raws = ctx.enter_context(tc.tile_pool(name="raws", bufs=AHEAD + 1))
+        groups = ctx.enter_context(tc.tile_pool(name="groups", bufs=4))
+        codes = ctx.enter_context(tc.tile_pool(name="codes", bufs=6))
+        psum = ctx.enter_context(tc.psum_pool(name="psum", bufs=4))
+
+        offs_t = keep.tile([P, S // 16], U16, name="offs_t")
+        pos_t = [keep.tile([P, T // 16], U16, name=f"pos_t{r}") for r in range(2)]
+        x_raw = [keep.tile([P, J, T], F32, name=f"x_raw{a}") for a in range(2)]
+        x_grp = [keep.tile([P, T, J], BF16, name=f"x_grp{a}", align_bytes=64) for a in range(2)]
+        x_codes = [keep.tile([P, T], U32, name=f"x_codes{a}", align_bytes=64) for a in range(2)]
+        x_scales = keep.tile([P, T], U8, name="x_scales", align_bytes=64)
+        s_codes = [keep.tile([P, S], U32, name=f"s_codes{a}", align_bytes=64) for a in range(2)]
+        s_scales = keep.tile([P, S], U8, name="s_scales", align_bytes=64)
+        bias = keep.tile([P, TT, E], F32, name="bias")
+        y = [keep.tile([P, S], F32, name=f"y{t}") for t in range(TT)]
+        gates = [keep.tile([P, T], F32, name=f"gate{r}") for r in range(2)]
+        wp_raw = keep.tile([P, TT, M], F32, name="wp_raw")
+        wp_grp = keep.tile([P, M, TT], BF16, name="wp_grp", align_bytes=64)
+        wp_codes = keep.tile([P, M], U32, name="wp_codes", align_bytes=64)
+        wp_scales = keep.tile([P, M], U8, name="wp_scales", align_bytes=64)
+        c_codes = keep.tile([P, T], U32, name="c_codes", align_bytes=64)
+        c_scales = keep.tile([P, T], U8, name="c_scales", align_bytes=64)
+        warm = keep.tile([P, 1], F32, name="warm")
+        warm2 = keep.tile([P, 1], F32, name="warm2")
+
+        nc.gpsimd.memset(x_scales[:], 0)
+        nc.vector.memset(warm[:], 0.0)
+        nc.scalar.activation(warm2[:], warm[:], RELU)
+
+        for a in range(2):
+            nc.sync.dma_start(x_raw[a][:], xT[512 * a : 512 * a + 512, :].rearrange("(p j) t -> p j t", j=J))
+            if a == 0:
+                nc.sync.dma_start(offs_t[:], offs)
+
+        w_raw = {}
+
+        def load_piece(s):
+            e, a = divmod(s, 2)
+            rows = w[e, 512 * a : 512 * a + 512, :].rearrange("(p j) n -> p j n", j=J)
+            step = 2 if s == PIECES - 1 else 4
+            parts = []
+            for j in range(0, J, step):
+                raw = raws.tile([P, step, N], F32, name="w_raw")
+                nc.sync.dma_start(raw[:], rows[:, j : j + step, :])
+                parts.append(raw)
+            w_raw[s] = parts
+
+        load_piece(0)
+        for i in range(I):
+            nc.sync.dma_start(bias[i:P:I, :, :], b.rearrange("(g t i) e -> i g t e", t=TT, i=I)[i])
+        for s in range(1, AHEAD):
+            load_piece(s)
+        nc.sync.dma_start(pos_t[0][:], pos1)
+        nc.sync.dma_start(pos_t[1][:], pos2)
+
+        def copy_on(scalar, out, in_):
+            if scalar:
+                nc.scalar.copy(out, in_)
+            else:
+                nc.vector.tensor_copy(out, in_)
+
+        def interleave_x(a):
+            o = x_grp[a][:].rearrange("p (c i) j -> p c j i", i=4)
+            v = x_raw[a][:].rearrange("p j (c i) -> p c j i", i=4)
+            copy_on(False, o[:, 0:64], v[:, 0:64])
+            copy_on(True, o[:, 64:128], v[:, 64:128])
+
+        def quantize_x(a):
+            nc.vector.quantize_mx(
+                out=x_codes[a][:].bitcast(FP8X4), scales=x_scales[4 * a : P, :], in_=x_grp[a][:].rearrange("p t j -> p (t j)")
+            )
+
+        def gather_slots(lo, hi):
+            idx = offs_t[:, lo // 16 : hi // 16]
+            for a in range(2):
+                nc.vector.tensor_copy(s_codes[a][:, lo:hi], x_codes[a][:].indirect(idx))
+            nc.vector.tensor_copy(s_scales[:, lo:hi], x_scales[:].indirect(idx))
+
+        w_grp = {}
+        w_codes = {}
+
+        def interleave_piece(s):
+            grp = groups.tile([P, TT, G, I, J], BF16, name="w_grp", align_bytes=64)
+            parts = w_raw.pop(s)
+            step = J // len(parts)
+            for j, raw in zip(range(0, J, step), parts):
+                o = grp[:, :, :, :, j : j + step].rearrange("p t g i j -> p t g j i")
+                v = raw[:].rearrange("p j (g t i) -> p t g j i", t=TT, i=I)
+                copy_on(False, o[:, 0:2], v[:, 0:2])
+                copy_on(True, o[:, 2:4], v[:, 2:4])
+            w_grp[s] = grp
+
+        def quantize_piece(s):
+            cod = codes.tile([P, N], U32, name="w_cod", align_bytes=64)
+            sca = codes.tile([P, N], U8, name="w_sca", align_bytes=64)
+            flat = w_grp.pop(s)[:].rearrange("p t g i j -> p (t g i j)")
+            step = 2 if s == PIECES - 1 else 4
+            for t in range(0, TT, step):
+                cols = slice(P * t, P * (t + step))
+                nc.vector.quantize_mx(
+                    out=cod[:, cols].bitcast(FP8X4), scales=sca[:, cols], in_=flat[:, J * P * t : J * P * (t + step)]
+                )
+            w_codes[s] = (cod, sca)
+
+        def expert(e):
+            slots = slice(C * e, C * e + C)
+            halves = [w_codes.pop(2 * e + a) for a in range(2)]
+            if e < E - 1:
+                bank = psum.tile([P, TT, C], F32, name="y_bank")
+                sums = [bank[:, t, :] for t in range(TT)]
+            else:
+                sums = []
+                for t in range(TT):
+                    bank = psum.tile([P, C], F32, name="y_bank")
+                    sums.append(bank[:])
+            for t in range(TT):
+                cols = slice(P * t, P * t + P)
+                for a in range(2):
+                    nc.tensor.matmul_mx(
+                        out=sums[t],
+                        lhsT=halves[a][0][:, cols].bitcast(FP8X4),
+                        lhsT_scale=halves[a][1][:, cols],
+                        rhs=s_codes[a][:, slots].bitcast(FP8X4),
+                        rhs_scale=s_scales[4 * a : P, slots],
+                        start=(a == 0),
+                        stop=(a == 1),
+                    )
+            for t in range(TT):
+                nc.scalar.activation(y[t][:, slots], sums[t], RELU, bias=bias[:, t, e : e + 1])
+
+        interleave_x(0)
+        interleave_x(1)
+        quantize_x(0)
+        quantize_x(1)
+        gather_slots(*SLOT_CUTS[0])
+        for s in range(PIECES + 1):
+            if s + AHEAD < PIECES:
+                load_piece(s + AHEAD)
+            elif s + AHEAD == PIECES:
+                for r in range(2):
+                    nc.sync.dma_start(gates[r][:], gate[r, 0:P, :])
+                for i in range(I):
+                    nc.sync.dma_start(wp_raw[i:P:I, :, :], wp.rearrange("(g t i) f -> i g t f", t=TT, i=I)[i])
+            if s < PIECES:
+                interleave_piece(s)
+            if s > 0:
+                quantize_piece(s - 1)
+                if s % 2 == 0:
+                    expert(s // 2 - 1)
+            if s == 2:
+                gather_slots(*SLOT_CUTS[1])
+            if s == 5:
+                gather_slots(*SLOT_CUTS[2])
+
+        nc.scalar.copy(wp_grp[:].rearrange("p (c i) t -> p c t i", i=4), wp_raw[:].rearrange("p t (c i) -> p c t i", i=4))
+
+        prods = {}
+
+        def gather_results(q, t):
+            lo, hi = TOKEN_CUTS[q]
+            for r in range(2):
+                if t == 0:
+                    prods[q, r] = keep.tile([P, TT, hi - lo], F32, name=f"prod{q}{r}")
+                nc.vector.tensor_tensor(
+                    prods[q, r][:, t, :],
+                    y[t][:].indirect(pos_t[r][:, lo // 16 : hi // 16]),
+                    gates[r][:, lo:hi],
+                    MULT,
+                )
+
+        def combine(q):
+            lo, hi = TOKEN_CUTS[q]
+            c_grp = keep.tile([P, hi - lo, TT], BF16, name=f"c_grp{q}", align_bytes=64)
+            nc.vector.tensor_tensor(
+                c_grp[:].rearrange("p (c i) t -> p c t i", i=4),
+                prods[q, 0][:].rearrange("p t (c i) -> p c t i", i=4),
+                prods[q, 1][:].rearrange("p t (c i) -> p c t i", i=4),
+                ADD,
+            )
+            return c_grp
+
+        def quantize_c(q, c_grp):
+            lo0 = TOKEN_CUTS[q][0]
+            flat = c_grp[:].rearrange("p n t -> p (n t)")
+            for lo, n in RUNS[q]:
+                nc.vector.quantize_mx(
+                    out=c_codes[:, lo : lo + n].bitcast(FP8X4),
+                    scales=c_scales[:, lo : lo + n],
+                    in_=flat[:, TT * (lo - lo0) : TT * (lo - lo0 + n)],
+                )
+
+        def project(q):
+            lo0, hi0 = TOKEN_CUTS[q]
+            res = keep.tile([P, 2, hi0 - lo0], F32, name=f"res{q}")
+            for m in range(2):
+                bank = psum.tile([P, hi0 - lo0], F32, name="o_bank")
+                for lo, n in RUNS[q]:
+                    nc.tensor.matmul_mx(
+                        out=bank[:, lo - lo0 : lo - lo0 + n],
+                        lhsT=wp_codes[:, P * m : P * m + P].bitcast(FP8X4),
+                        lhsT_scale=wp_scales[:, P * m : P * m + P],
+                        rhs=c_codes[:, lo : lo + n].bitcast(FP8X4),
+                        rhs_scale=c_scales[:, lo : lo + n],
+                        start=True,
+                        stop=True,
+                    )
+                copy_on(m == 0 or q == 0, res[:, m, :], bank[:])
+            nc.sync.dma_start(out.rearrange("(m p) t -> p m t", p=P)[:, :, lo0:hi0], res[:])
+
+        for t in range(TT):
+            gather_results(0, t)
+            if t == 1:
+                nc.vector.quantize_mx(
+                    out=wp_codes[:].bitcast(FP8X4), scales=wp_scales[:], in_=wp_grp[:].rearrange("p f t -> p (f t)")
+                )
+        gather_results(1, 0)
+        c0 = combine(0)
+        gather_results(1, 1)
+        quantize_c(0, c0)
+        project(0)
+        gather_results(1, 2)
+        gather_results(1, 3)
+        c1 = combine(1)
+        quantize_c(1, c1)
+        project(1)

@@ -115,6 +115,9 @@ def tile_moe_nxt_lin_relu_kernel(tc, xT, w, b, wp, gate, offs, pos1, pos2, out):
         w_grp = {}
         w_codes = {}
 
+        def vector_quarters(s):
+            return 1 if s < 4 else 2 + s % 2
+
         def interleave_piece(s):
             grp = groups.tile([P, TT, G, I, J], BF16, name="w_grp", align_bytes=64)
             parts = w_raw.pop(s)
@@ -122,8 +125,9 @@ def tile_moe_nxt_lin_relu_kernel(tc, xT, w, b, wp, gate, offs, pos1, pos2, out):
             for j, raw in zip(range(0, J, step), parts):
                 o = grp[:, :, :, :, j : j + step].rearrange("p t g i j -> p t g j i")
                 v = raw[:].rearrange("p j (g t i) -> p t g j i", t=TT, i=I)
-                copy_on(False, o[:, 0:2], v[:, 0:2])
-                copy_on(True, o[:, 2:4], v[:, 2:4])
+                cut = vector_quarters(s)
+                copy_on(False, o[:, 0:cut], v[:, 0:cut])
+                copy_on(True, o[:, cut:TT], v[:, cut:TT])
             w_grp[s] = grp
 
         def quantize_piece(s):

@@ -19,12 +19,15 @@ FP8X4 = mybir.dt.float8_e4m3fn_x4
 RELU = mybir.ActivationFunctionType.Relu
 MULT = mybir.AluOpType.mult
 ADD = mybir.AluOpType.add
+MAX = mybir.AluOpType.max
 
 FLOPS = 2 * S * K * N + 2 * N * M * T
 BYTES = 4 * (K * T + E * K * N + N * E + N * M + 2 * T + M * T) + 2 * P * (S + 2 * T) // 16
 
 PIECES = 2 * E
 AHEAD = 10
+VECTOR_QUARTERS = (1, 2, 0, 0, 2, 0, 4, 1, 4, 1, 2, 4, 1, 2, 4, 2)
+RELU_ON = "VVVVSVSS"
 SLOT_CUTS = ((0, 384), (384, 768), (768, 1024))
 TOKEN_CUTS = ((0, 384), (384, 512))
 RUNS = (((0, 256), (256, 128)), ((384, 128),))
@@ -35,9 +38,9 @@ def tile_moe_nxt_lin_relu_kernel(tc, xT, w, b, wp, gate, offs, pos1, pos2, out):
     with ExitStack() as ctx:
         keep = ctx.enter_context(tc.tile_pool(name="keep", bufs=1))
         raws = ctx.enter_context(tc.tile_pool(name="raws", bufs=AHEAD + 1))
-        groups = ctx.enter_context(tc.tile_pool(name="groups", bufs=4))
-        codes = ctx.enter_context(tc.tile_pool(name="codes", bufs=6))
-        psum = ctx.enter_context(tc.psum_pool(name="psum", bufs=4))
+        groups = ctx.enter_context(tc.tile_pool(name="groups", bufs=6))
+        codes = ctx.enter_context(tc.tile_pool(name="codes", bufs=10))
+        psum = ctx.enter_context(tc.psum_pool(name="psum", bufs=8))
 
         offs_t = keep.tile([P, S // 16], U16, name="offs_t")
         pos_t = [keep.tile([P, T // 16], U16, name=f"pos_t{r}") for r in range(2)]
@@ -49,8 +52,6 @@ def tile_moe_nxt_lin_relu_kernel(tc, xT, w, b, wp, gate, offs, pos1, pos2, out):
         s_scales = keep.tile([P, S], U8, name="s_scales", align_bytes=64)
         bias = keep.tile([P, TT, E], F32, name="bias")
         y = [keep.tile([P, S], F32, name=f"y{t}") for t in range(TT)]
-        gates = [keep.tile([P, T], F32, name=f"gate{r}") for r in range(2)]
-        wp_raw = keep.tile([P, TT, M], F32, name="wp_raw")
         wp_grp = keep.tile([P, M, TT], BF16, name="wp_grp", align_bytes=64)
         wp_codes = keep.tile([P, M], U32, name="wp_codes", align_bytes=64)
         wp_scales = keep.tile([P, M], U8, name="wp_scales", align_bytes=64)
@@ -115,9 +116,6 @@ def tile_moe_nxt_lin_relu_kernel(tc, xT, w, b, wp, gate, offs, pos1, pos2, out):
         w_grp = {}
         w_codes = {}
 
-        def vector_quarters(s):
-            return 1 if s < 4 else 2 + s % 2
-
         def interleave_piece(s):
             grp = groups.tile([P, TT, G, I, J], BF16, name="w_grp", align_bytes=64)
             parts = w_raw.pop(s)
@@ -125,34 +123,31 @@ def tile_moe_nxt_lin_relu_kernel(tc, xT, w, b, wp, gate, offs, pos1, pos2, out):
             for j, raw in zip(range(0, J, step), parts):
                 o = grp[:, :, :, :, j : j + step].rearrange("p t g i j -> p t g j i")
                 v = raw[:].rearrange("p j (g t i) -> p t g j i", t=TT, i=I)
-                cut = vector_quarters(s)
-                copy_on(False, o[:, 0:cut], v[:, 0:cut])
-                copy_on(True, o[:, cut:TT], v[:, cut:TT])
+                cut = VECTOR_QUARTERS[s]
+                if cut:
+                    copy_on(False, o[:, 0:cut], v[:, 0:cut])
+                if cut < TT:
+                    copy_on(True, o[:, cut:TT], v[:, cut:TT])
             w_grp[s] = grp
 
         def quantize_piece(s):
             cod = codes.tile([P, N], U32, name="w_cod", align_bytes=64)
             sca = codes.tile([P, N], U8, name="w_sca", align_bytes=64)
             flat = w_grp.pop(s)[:].rearrange("p t g i j -> p (t g i j)")
-            step = 2 if s == PIECES - 1 else 4
-            for t in range(0, TT, step):
-                cols = slice(P * t, P * (t + step))
+            for lo, hi in ((0, 1), (1, 2), (2, 4)) if s == PIECES - 1 else ((0, 4),):
+                cols = slice(P * lo, P * hi)
                 nc.vector.quantize_mx(
-                    out=cod[:, cols].bitcast(FP8X4), scales=sca[:, cols], in_=flat[:, J * P * t : J * P * (t + step)]
+                    out=cod[:, cols].bitcast(FP8X4), scales=sca[:, cols], in_=flat[:, J * P * lo : J * P * hi]
                 )
             w_codes[s] = (cod, sca)
 
         def expert(e):
             slots = slice(C * e, C * e + C)
             halves = [w_codes.pop(2 * e + a) for a in range(2)]
-            if e < E - 1:
-                bank = psum.tile([P, TT, C], F32, name="y_bank")
-                sums = [bank[:, t, :] for t in range(TT)]
-            else:
-                sums = []
-                for t in range(TT):
-                    bank = psum.tile([P, C], F32, name="y_bank")
-                    sums.append(bank[:])
+            sums = []
+            for t in range(TT):
+                bank = psum.tile([P, C], F32, name="bank")
+                sums.append(bank[:])
             for t in range(TT):
                 cols = slice(P * t, P * t + P)
                 for a in range(2):
@@ -166,7 +161,10 @@ def tile_moe_nxt_lin_relu_kernel(tc, xT, w, b, wp, gate, offs, pos1, pos2, out):
                         stop=(a == 1),
                     )
             for t in range(TT):
-                nc.scalar.activation(y[t][:, slots], sums[t], RELU, bias=bias[:, t, e : e + 1])
+                if RELU_ON[e] == "V" or (RELU_ON[e] == "M" and t >= 2):
+                    nc.vector.tensor_scalar(y[t][:, slots], sums[t], bias[:, t, e : e + 1], 0.0, ADD, MAX)
+                else:
+                    nc.scalar.activation(y[t][:, slots], sums[t], RELU, bias=bias[:, t, e : e + 1])
 
         interleave_x(0)
         interleave_x(1)
@@ -177,8 +175,10 @@ def tile_moe_nxt_lin_relu_kernel(tc, xT, w, b, wp, gate, offs, pos1, pos2, out):
             if s + AHEAD < PIECES:
                 load_piece(s + AHEAD)
             elif s + AHEAD == PIECES:
+                gates = raws.tile([P, 2, T], F32, name="w_raw")
                 for r in range(2):
-                    nc.sync.dma_start(gates[r][:], gate[r, 0:P, :])
+                    nc.sync.dma_start(gates[:, r, :], gate[r, 0:P, :])
+                wp_raw = raws.tile([P, TT, M], F32, name="w_raw")
                 for i in range(I):
                     nc.sync.dma_start(wp_raw[i:P:I, :, :], wp.rearrange("(g t i) f -> i g t f", t=TT, i=I)[i])
             if s < PIECES:
@@ -194,17 +194,14 @@ def tile_moe_nxt_lin_relu_kernel(tc, xT, w, b, wp, gate, offs, pos1, pos2, out):
 
         nc.scalar.copy(wp_grp[:].rearrange("p (c i) t -> p c t i", i=4), wp_raw[:].rearrange("p t (c i) -> p c t i", i=4))
 
-        prods = {}
+        prods = [keep.tile([P, TT, T], F32, name=f"prod{r}") for r in range(2)]
 
-        def gather_results(q, t):
-            lo, hi = TOKEN_CUTS[q]
-            for r in range(2):
-                if t == 0:
-                    prods[q, r] = keep.tile([P, TT, hi - lo], F32, name=f"prod{q}{r}")
+        def gather_results(t, lo, hi, rs=(0, 1)):
+            for r in rs:
                 nc.vector.tensor_tensor(
-                    prods[q, r][:, t, :],
+                    prods[r][:, t, lo:hi],
                     y[t][:].indirect(pos_t[r][:, lo // 16 : hi // 16]),
-                    gates[r][:, lo:hi],
+                    gates[:, r, lo:hi],
                     MULT,
                 )
 
@@ -213,8 +210,8 @@ def tile_moe_nxt_lin_relu_kernel(tc, xT, w, b, wp, gate, offs, pos1, pos2, out):
             c_grp = keep.tile([P, hi - lo, TT], BF16, name=f"c_grp{q}", align_bytes=64)
             nc.vector.tensor_tensor(
                 c_grp[:].rearrange("p (c i) t -> p c t i", i=4),
-                prods[q, 0][:].rearrange("p t (c i) -> p c t i", i=4),
-                prods[q, 1][:].rearrange("p t (c i) -> p c t i", i=4),
+                prods[0][:, :, lo:hi].rearrange("p t (c i) -> p c t i", i=4),
+                prods[1][:, :, lo:hi].rearrange("p t (c i) -> p c t i", i=4),
                 ADD,
             )
             return c_grp
@@ -232,11 +229,18 @@ def tile_moe_nxt_lin_relu_kernel(tc, xT, w, b, wp, gate, offs, pos1, pos2, out):
         def project(q):
             lo0, hi0 = TOKEN_CUTS[q]
             res = keep.tile([P, 2, hi0 - lo0], F32, name=f"res{q}")
+            rows = out.rearrange("(m p) t -> p m t", p=P)
+            if q == 1:
+                both = psum.tile([P, 2, hi0 - lo0], F32, name="bank")
             for m in range(2):
-                bank = psum.tile([P, hi0 - lo0], F32, name="o_bank")
+                if q == 1:
+                    sums = both[:, m, :]
+                else:
+                    bank = psum.tile([P, hi0 - lo0], F32, name="bank")
+                    sums = bank[:]
                 for lo, n in RUNS[q]:
                     nc.tensor.matmul_mx(
-                        out=bank[:, lo - lo0 : lo - lo0 + n],
+                        out=sums[:, lo - lo0 : lo - lo0 + n],
                         lhsT=wp_codes[:, P * m : P * m + P].bitcast(FP8X4),
                         lhsT_scale=wp_scales[:, P * m : P * m + P],
                         rhs=c_codes[:, lo : lo + n].bitcast(FP8X4),
@@ -244,22 +248,25 @@ def tile_moe_nxt_lin_relu_kernel(tc, xT, w, b, wp, gate, offs, pos1, pos2, out):
                         start=True,
                         stop=True,
                     )
-                copy_on(m == 0 or q == 0, res[:, m, :], bank[:])
-            nc.sync.dma_start(out.rearrange("(m p) t -> p m t", p=P)[:, :, lo0:hi0], res[:])
+                if q == 0:
+                    nc.scalar.copy(res[:, m, :], sums)
+                    nc.sync.dma_start(rows[:, m, lo0:hi0], res[:, m, :])
+            if q == 1:
+                nc.vector.tensor_copy(res[:], both[:])
+                nc.sync.dma_start(rows[:, :, lo0:hi0], res[:])
 
-        for t in range(TT):
-            gather_results(0, t)
+        for t in range(TT - 1):
+            gather_results(t, 0, T)
             if t == 1:
                 nc.vector.quantize_mx(
                     out=wp_codes[:].bitcast(FP8X4), scales=wp_scales[:], in_=wp_grp[:].rearrange("p f t -> p (f t)")
                 )
-        gather_results(1, 0)
+        gather_results(TT - 1, 0, 384)
+        gather_results(TT - 1, 384, T, (0,))
         c0 = combine(0)
-        gather_results(1, 1)
+        gather_results(TT - 1, 384, T, (1,))
         quantize_c(0, c0)
         project(0)
-        gather_results(1, 2)
-        gather_results(1, 3)
         c1 = combine(1)
         quantize_c(1, c1)
         project(1)

@@ -26,8 +26,8 @@ BYTES = 4 * (K * T + E * K * N + N * E + N * M + 2 * T + M * T) + 2 * P * (S + 2
 
 PIECES = 2 * E
 AHEAD = 10
-VECTOR_QUARTERS = (1, 2, 0, 0, 2, 0, 4, 1, 4, 1, 2, 4, 1, 2, 4, 2)
-RELU_ON = "VVVVSVSS"
+VECTOR_QUARTERS = (0, 1, 0, 0, 4, 1, 0, 4, 4, 0, 2, 1, 4, 1, 2, 2)
+RELU_ON = "VVSVVVSS"
 SLOT_CUTS = ((0, 384), (384, 768), (768, 1024))
 TOKEN_CUTS = ((0, 384), (384, 512))
 RUNS = (((0, 256), (256, 128)), ((384, 128),))
@@ -99,8 +99,7 @@ def tile_moe_nxt_lin_relu_kernel(tc, xT, w, b, wp, gate, offs, pos1, pos2, out):
         def interleave_x(a):
             o = x_grp[a][:].rearrange("p (c i) j -> p c j i", i=4)
             v = x_raw[a][:].rearrange("p j (c i) -> p c j i", i=4)
-            copy_on(False, o[:, 0:64], v[:, 0:64])
-            copy_on(True, o[:, 64:128], v[:, 64:128])
+            copy_on(True, o, v)
 
         def quantize_x(a):
             nc.vector.quantize_mx(

from contextlib import ExitStack

import concourse.mybir as mybir

E, K, N, T, C, M = 8, 1024, 512, 512, 128, 256
S = E * C
P = 128
J = 4
TT = 4
G = 32
I = 4

F32 = mybir.dt.float32
BF16 = mybir.dt.bfloat16
U32 = mybir.dt.uint32
U16 = mybir.dt.uint16
U8 = mybir.dt.uint8
FP8X4 = mybir.dt.float8_e4m3fn_x4
RELU = mybir.ActivationFunctionType.Relu
MULT = mybir.AluOpType.mult
ADD = mybir.AluOpType.add
MAX = mybir.AluOpType.max

FLOPS = 2 * S * K * N + 2 * N * M * T
BYTES = 4 * (K * T + E * K * N + N * E + N * M + 2 * T + M * T) + 2 * P * (S + 2 * T) // 16

PIECES = 2 * E
AHEAD = 10
VECTOR_QUARTERS = (0, 1, 0, 0, 4, 1, 0, 4, 4, 0, 2, 1, 4, 1, 2, 2)
RELU_ON = "VVSVVVSS"
SLOT_CUTS = ((0, 384), (384, 768), (768, 1024))
TOKEN_CUTS = ((0, 384), (384, 512))
RUNS = (((0, 256), (256, 128)), ((384, 128),))


def tile_moe_nxt_lin_relu_kernel(tc, xT, w, b, wp, gate, offs, pos1, pos2, out):
    nc = tc.nc
    with ExitStack() as ctx:
        keep = ctx.enter_context(tc.tile_pool(name="keep", bufs=1))
        raws = ctx.enter_context(tc.tile_pool(name="raws", bufs=AHEAD + 1))
        groups = ctx.enter_context(tc.tile_pool(name="groups", bufs=6))
        codes = ctx.enter_context(tc.tile_pool(name="codes", bufs=10))
        psum = ctx.enter_context(tc.psum_pool(name="psum", bufs=8))

        offs_t = keep.tile([P, S // 16], U16, name="offs_t")
        pos_t = [keep.tile([P, T // 16], U16, name=f"pos_t{r}") for r in range(2)]
        x_raw = [keep.tile([P, J, T], F32, name=f"x_raw{a}") for a in range(2)]
        x_grp = [keep.tile([P, T, J], BF16, name=f"x_grp{a}", align_bytes=64) for a in range(2)]
        x_codes = [keep.tile([P, T], U32, name=f"x_codes{a}", align_bytes=64) for a in range(2)]
        x_scales = keep.tile([P, T], U8, name="x_scales", align_bytes=64)
        s_codes = [keep.tile([P, S], U32, name=f"s_codes{a}", align_bytes=64) for a in range(2)]
        s_scales = keep.tile([P, S], U8, name="s_scales", align_bytes=64)
        bias = keep.tile([P, TT, E], F32, name="bias")
        y = [keep.tile([P, S], F32, name=f"y{t}") for t in range(TT)]
        wp_grp = keep.tile([P, M, TT], BF16, name="wp_grp", align_bytes=64)
        wp_codes = keep.tile([P, M], U32, name="wp_codes", align_bytes=64)
        wp_scales = keep.tile([P, M], U8, name="wp_scales", align_bytes=64)
        c_codes = keep.tile([P, T], U32, name="c_codes", align_bytes=64)
        c_scales = keep.tile([P, T], U8, name="c_scales", align_bytes=64)
        warm = keep.tile([P, 1], F32, name="warm")
        warm2 = keep.tile([P, 1], F32, name="warm2")

        nc.gpsimd.memset(x_scales[:], 0)
        nc.vector.memset(warm[:], 0.0)
        nc.scalar.activation(warm2[:], warm[:], RELU)

        for a in range(2):
            nc.sync.dma_start(x_raw[a][:], xT[512 * a : 512 * a + 512, :].rearrange("(p j) t -> p j t", j=J))
            if a == 0:
                nc.sync.dma_start(offs_t[:], offs)

        w_raw = {}

        def load_piece(s):
            e, a = divmod(s, 2)
            rows = w[e, 512 * a : 512 * a + 512, :].rearrange("(p j) n -> p j n", j=J)
            step = 2 if s == PIECES - 1 else 4
            parts = []
            for j in range(0, J, step):
                raw = raws.tile([P, step, N], F32, name="w_raw")
                nc.sync.dma_start(raw[:], rows[:, j : j + step, :])
                parts.append(raw)
            w_raw[s] = parts

        load_piece(0)
        for i in range(I):
            nc.sync.dma_start(bias[i:P:I, :, :], b.rearrange("(g t i) e -> i g t e", t=TT, i=I)[i])
        for s in range(1, AHEAD):
            load_piece(s)
        nc.sync.dma_start(pos_t[0][:], pos1)
        nc.sync.dma_start(pos_t[1][:], pos2)

        def copy_on(scalar, out, in_):
            if scalar:
                nc.scalar.copy(out, in_)
            else:
                nc.vector.tensor_copy(out, in_)

        def interleave_x(a):
            o = x_grp[a][:].rearrange("p (c i) j -> p c j i", i=4)
            v = x_raw[a][:].rearrange("p j (c i) -> p c j i", i=4)
            copy_on(True, o, v)

        def quantize_x(a):
            nc.vector.quantize_mx(
                out=x_codes[a][:].bitcast(FP8X4), scales=x_scales[4 * a : P, :], in_=x_grp[a][:].rearrange("p t j -> p (t j)")
            )

        def gather_slots(lo, hi):
            idx = offs_t[:, lo // 16 : hi // 16]
            for a in range(2):
                nc.vector.tensor_copy(s_codes[a][:, lo:hi], x_codes[a][:].indirect(idx))
            nc.vector.tensor_copy(s_scales[:, lo:hi], x_scales[:].indirect(idx))

        w_grp = {}
        w_codes = {}

        def interleave_piece(s):
            grp = groups.tile([P, TT, G, I, J], BF16, name="w_grp", align_bytes=64)
            parts = w_raw.pop(s)
            step = J // len(parts)
            for j, raw in zip(range(0, J, step), parts):
                o = grp[:, :, :, :, j : j + step].rearrange("p t g i j -> p t g j i")
                v = raw[:].rearrange("p j (g t i) -> p t g j i", t=TT, i=I)
                cut = VECTOR_QUARTERS[s]
                if cut:
                    copy_on(False, o[:, 0:cut], v[:, 0:cut])
                if cut < TT:
                    copy_on(True, o[:, cut:TT], v[:, cut:TT])
            w_grp[s] = grp

        def quantize_piece(s):
            cod = codes.tile([P, N], U32, name="w_cod", align_bytes=64)
            sca = codes.tile([P, N], U8, name="w_sca", align_bytes=64)
            flat = w_grp.pop(s)[:].rearrange("p t g i j -> p (t g i j)")
            for lo, hi in ((0, 1), (1, 2), (2, 4)) if s == PIECES - 1 else ((0, 4),):
                cols = slice(P * lo, P * hi)
                nc.vector.quantize_mx(
                    out=cod[:, cols].bitcast(FP8X4), scales=sca[:, cols], in_=flat[:, J * P * lo : J * P * hi]
                )
            w_codes[s] = (cod, sca)

        def expert(e):
            slots = slice(C * e, C * e + C)
            halves = [w_codes.pop(2 * e + a) for a in range(2)]
            sums = []
            for t in range(TT):
                bank = psum.tile([P, C], F32, name="bank")
                sums.append(bank[:])
            for t in range(TT):
                cols = slice(P * t, P * t + P)
                for a in range(2):
                    nc.tensor.matmul_mx(
                        out=sums[t],
                        lhsT=halves[a][0][:, cols].bitcast(FP8X4),
                        lhsT_scale=halves[a][1][:, cols],
                        rhs=s_codes[a][:, slots].bitcast(FP8X4),
                        rhs_scale=s_scales[4 * a : P, slots],
                        start=(a == 0),
                        stop=(a == 1),
                    )
            for t in range(TT):
                if RELU_ON[e] == "V" or (RELU_ON[e] == "M" and t >= 2):
                    nc.vector.tensor_scalar(y[t][:, slots], sums[t], bias[:, t, e : e + 1], 0.0, ADD, MAX)
                else:
                    nc.scalar.activation(y[t][:, slots], sums[t], RELU, bias=bias[:, t, e : e + 1])

        interleave_x(0)
        interleave_x(1)
        quantize_x(0)
        quantize_x(1)
        gather_slots(*SLOT_CUTS[0])
        for s in range(PIECES + 1):
            if s + AHEAD < PIECES:
                load_piece(s + AHEAD)
            elif s + AHEAD == PIECES:
                gates = raws.tile([P, 2, T], F32, name="w_raw")
                for r in range(2):
                    nc.sync.dma_start(gates[:, r, :], gate[r, 0:P, :])
                wp_raw = raws.tile([P, TT, M], F32, name="w_raw")
                for i in range(I):
                    nc.sync.dma_start(wp_raw[i:P:I, :, :], wp.rearrange("(g t i) f -> i g t f", t=TT, i=I)[i])
            if s < PIECES:
                interleave_piece(s)
            if s > 0:
                quantize_piece(s - 1)
                if s % 2 == 0:
                    expert(s // 2 - 1)
            if s == 2:
                gather_slots(*SLOT_CUTS[1])
            if s == 5:
                gather_slots(*SLOT_CUTS[2])

        nc.scalar.copy(wp_grp[:].rearrange("p (c i) t -> p c t i", i=4), wp_raw[:].rearrange("p t (c i) -> p c t i", i=4))

        prods = [keep.tile([P, TT, T], F32, name=f"prod{r}") for r in range(2)]

        def gather_results(t, lo, hi, rs=(0, 1)):
            for r in rs:
                nc.vector.tensor_tensor(
                    prods[r][:, t, lo:hi],
                    y[t][:].indirect(pos_t[r][:, lo // 16 : hi // 16]),
                    gates[:, r, lo:hi],
                    MULT,
                )

        def combine(q):
            lo, hi = TOKEN_CUTS[q]
            c_grp = keep.tile([P, hi - lo, TT], BF16, name=f"c_grp{q}", align_bytes=64)
            nc.vector.tensor_tensor(
                c_grp[:].rearrange("p (c i) t -> p c t i", i=4),
                prods[0][:, :, lo:hi].rearrange("p t (c i) -> p c t i", i=4),
                prods[1][:, :, lo:hi].rearrange("p t (c i) -> p c t i", i=4),
                ADD,
            )
            return c_grp

        def quantize_c(q, c_grp):
            lo0 = TOKEN_CUTS[q][0]
            flat = c_grp[:].rearrange("p n t -> p (n t)")
            for lo, n in RUNS[q]:
                nc.vector.quantize_mx(
                    out=c_codes[:, lo : lo + n].bitcast(FP8X4),
                    scales=c_scales[:, lo : lo + n],
                    in_=flat[:, TT * (lo - lo0) : TT * (lo - lo0 + n)],
                )

        def project(q):
            lo0, hi0 = TOKEN_CUTS[q]
            res = keep.tile([P, 2, hi0 - lo0], F32, name=f"res{q}")
            rows = out.rearrange("(m p) t -> p m t", p=P)
            if q == 1:
                both = psum.tile([P, 2, hi0 - lo0], F32, name="bank")
            for m in range(2):
                if q == 1:
                    sums = both[:, m, :]
                else:
                    bank = psum.tile([P, hi0 - lo0], F32, name="bank")
                    sums = bank[:]
                for lo, n in RUNS[q]:
                    nc.tensor.matmul_mx(
                        out=sums[:, lo - lo0 : lo - lo0 + n],
                        lhsT=wp_codes[:, P * m : P * m + P].bitcast(FP8X4),
                        lhsT_scale=wp_scales[:, P * m : P * m + P],
                        rhs=c_codes[:, lo : lo + n].bitcast(FP8X4),
                        rhs_scale=c_scales[:, lo : lo + n],
                        start=True,
                        stop=True,
                    )
                if q == 0:
                    nc.scalar.copy(res[:, m, :], sums)
                    nc.sync.dma_start(rows[:, m, lo0:hi0], res[:, m, :])
            if q == 1:
                nc.vector.tensor_copy(res[:], both[:])
                nc.sync.dma_start(rows[:, :, lo0:hi0], res[:])

        for t in range(TT - 1):
            gather_results(t, 0, T)
            if t == 1:
                nc.vector.quantize_mx(
                    out=wp_codes[:].bitcast(FP8X4), scales=wp_scales[:], in_=wp_grp[:].rearrange("p f t -> p (f t)")
                )
        gather_results(TT - 1, 0, 384)
        gather_results(TT - 1, 384, T, (0,))
        c0 = combine(0)
        gather_results(TT - 1, 384, T, (1,))
        quantize_c(0, c0)
        project(0)
        c1 = combine(1)
        quantize_c(1, c1)
        project(1)
